import numpy as np
import ml_dtypes

BF16 = ml_dtypes.bfloat16


def bf(x):
    return np.asarray(x, np.float32).astype(BF16)


def f32(x):
    return np.asarray(x, np.float32)


def f64(x):
    return np.asarray(x).astype(np.float64)


def striped(idx):
    return np.tile(idx.reshape(-1, 16).T, (8, 1))


def rows(idx, k):
    return np.tile(idx, (k, 1))


def look(tab, idx):
    return np.take_along_axis(f64(tab), rows(idx, len(tab)), axis=1)


K, S, V, N = 512, 2048, 2048, 2048


def setup_inputs():
    return {"tab": f32(np.random.standard_normal((K, S))), "y": f32(np.random.standard_normal((K, V))), "offs": striped(np.random.permutation(S)[:N])}


def reference(tab, y, offs):
    idx = offs[:16].T.reshape(-1)
    t = look(tab, idx)
    x = np.tanh(t) * f64(y)
    return x

@@ -1,0 +1,46 @@
+import concourse.mybir as mybir
+
+P = 128
+PIECE = 1024
+ENTRIES_PER_OFFSET_COLUMN = 16
+
+TANH = mybir.ActivationFunctionType.Tanh
+MULT = mybir.AluOpType.mult
+
+
+def tile_lookup_gate_tanh_out_kernel(tc, tab, y, offs, out):
+    nc = tc.nc
+    rows, table_columns = tab.shape
+    n = y.shape[1]
+    n_blocks = rows // P
+    f32 = mybir.dt.float32
+
+    with (
+        tc.tile_pool(name="lists", bufs=1) as lists,
+        tc.tile_pool(name="blocks", bufs=n_blocks) as blocks,
+    ):
+        offsets = lists.tile([P, n // ENTRIES_PER_OFFSET_COLUMN], mybir.dt.uint16, name="offsets")
+        nc.sync.dma_start(offsets[:], offs)
+
+        tables, streams = [], []
+        for b in range(n_blocks):
+            block_rows = slice(b * P, (b + 1) * P)
+            table = blocks.tile([P, table_columns], f32, name="table")
+            nc.sync.dma_start(table[:], tab[block_rows, :])
+            stream = blocks.tile([P, n], f32, name="stream")
+            nc.sync.dma_start(stream[:], y[block_rows, :])
+            tables.append(table)
+            streams.append(stream)
+
+        for b in range(n_blocks):
+            block_rows = slice(b * P, (b + 1) * P)
+            gate = blocks.tile([P, n], f32, name="gate")
+            product = blocks.tile([P, n], f32, name="product")
+            for start in range(0, n, PIECE):
+                cols = slice(start, start + PIECE)
+                piece_offsets = offsets[
+                    :, start // ENTRIES_PER_OFFSET_COLUMN : (start + PIECE) // ENTRIES_PER_OFFSET_COLUMN
+                ]
+                nc.scalar.activation(gate[:, cols], tables[b][:].indirect(piece_offsets), TANH)
+                nc.vector.tensor_tensor(product[:, cols], gate[:, cols], streams[b][:, cols], MULT)
+                nc.sync.dma_start(out[block_rows, cols], product[:, cols])

@@ -2,6 +2,7 @@ import concourse.mybir as mybir
 
 P = 128
 PIECE = 1024
+LAST_PIECE = PIECE // 2
 ENTRIES_PER_OFFSET_COLUMN = 16
 
 TANH = mybir.ActivationFunctionType.Tanh
@@ -36,10 +37,11 @@ def tile_lookup_gate_tanh_out_kernel(tc, tab, y, offs, out):
             block_rows = slice(b * P, (b + 1) * P)
             gate = blocks.tile([P, n], f32, name="gate")
             product = blocks.tile([P, n], f32, name="product")
-            for start in range(0, n, PIECE):
-                cols = slice(start, start + PIECE)
+            piece = LAST_PIECE if b == n_blocks - 1 else PIECE
+            for start in range(0, n, piece):
+                cols = slice(start, start + piece)
                 piece_offsets = offsets[
-                    :, start // ENTRIES_PER_OFFSET_COLUMN : (start + PIECE) // ENTRIES_PER_OFFSET_COLUMN
+                    :, start // ENTRIES_PER_OFFSET_COLUMN : (start + piece) // ENTRIES_PER_OFFSET_COLUMN
                 ]
                 nc.scalar.activation(gate[:, cols], tables[b][:].indirect(piece_offsets), TANH)
                 nc.vector.tensor_tensor(product[:, cols], gate[:, cols], streams[b][:, cols], MULT)

@@ -45,4 +45,7 @@ def tile_lookup_gate_tanh_out_kernel(tc, tab, y, offs, out):
                 ]
                 nc.scalar.activation(gate[:, cols], tables[b][:].indirect(piece_offsets), TANH)
                 nc.vector.tensor_tensor(product[:, cols], gate[:, cols], streams[b][:, cols], MULT)
-                nc.sync.dma_start(out[block_rows, cols], product[:, cols])
+                if b == n_blocks - 1:
+                    nc.sync.dma_start(out[block_rows, cols], product[:, cols])
+            if b < n_blocks - 1:
+                nc.sync.dma_start(out[block_rows, :], product[:])

@@ -4,6 +4,7 @@ P = 128
 PIECE = 1024
 LAST_PIECE = PIECE // 2
 ENTRIES_PER_OFFSET_COLUMN = 16
+BLOCKS_PER_PAIR = 2
 
 TANH = mybir.ActivationFunctionType.Tanh
 MULT = mybir.AluOpType.mult
@@ -14,38 +15,50 @@ def tile_lookup_gate_tanh_out_kernel(tc, tab, y, offs, out):
     rows, table_columns = tab.shape
     n = y.shape[1]
     n_blocks = rows // P
+    n_pairs = n_blocks // BLOCKS_PER_PAIR
     f32 = mybir.dt.float32
+
+    tab_rows = tab.rearrange("(p b) c -> p (b c)", b=n_blocks)
+    y_rows = y.rearrange("(p b) c -> p (b c)", b=n_blocks)
+    out_rows = out.rearrange("(p b) c -> p (b c)", b=n_blocks)
 
     with (
         tc.tile_pool(name="lists", bufs=1) as lists,
         tc.tile_pool(name="blocks", bufs=n_blocks) as blocks,
+        tc.tile_pool(name="pairs", bufs=n_pairs) as pairs,
     ):
         offsets = lists.tile([P, n // ENTRIES_PER_OFFSET_COLUMN], mybir.dt.uint16, name="offsets")
         nc.sync.dma_start(offsets[:], offs)
 
         tables, streams = [], []
-        for b in range(n_blocks):
-            block_rows = slice(b * P, (b + 1) * P)
-            table = blocks.tile([P, table_columns], f32, name="table")
-            nc.sync.dma_start(table[:], tab[block_rows, :])
-            stream = blocks.tile([P, n], f32, name="stream")
-            nc.sync.dma_start(stream[:], y[block_rows, :])
-            tables.append(table)
+        for pair in range(n_pairs):
+            for b in range(pair * BLOCKS_PER_PAIR, (pair + 1) * BLOCKS_PER_PAIR):
+                table = blocks.tile([P, table_columns], f32, name="table")
+                nc.sync.dma_start(table[:], tab_rows[:, b * table_columns : (b + 1) * table_columns])
+                tables.append(table)
+            stream = pairs.tile([P, BLOCKS_PER_PAIR * n], f32, name="stream")
+            pair_columns = slice(pair * BLOCKS_PER_PAIR * n, (pair + 1) * BLOCKS_PER_PAIR * n)
+            nc.sync.dma_start(stream[:], y_rows[:, pair_columns])
             streams.append(stream)
 
         for b in range(n_blocks):
-            block_rows = slice(b * P, (b + 1) * P)
             gate = blocks.tile([P, n], f32, name="gate")
             product = blocks.tile([P, n], f32, name="product")
-            piece = LAST_PIECE if b == n_blocks - 1 else PIECE
+            stream = streams[b // BLOCKS_PER_PAIR]
+            stream_start = (b % BLOCKS_PER_PAIR) * n
+            is_last = b == n_blocks - 1
+            piece = LAST_PIECE if is_last else PIECE
             for start in range(0, n, piece):
-                cols = slice(start, start + piece)
-                piece_offsets = offsets[
-                    :, start // ENTRIES_PER_OFFSET_COLUMN : (start + piece) // ENTRIES_PER_OFFSET_COLUMN
-                ]
-                nc.scalar.activation(gate[:, cols], tables[b][:].indirect(piece_offsets), TANH)
-                nc.vector.tensor_tensor(product[:, cols], gate[:, cols], streams[b][:, cols], MULT)
-                if b == n_blocks - 1:
-                    nc.sync.dma_start(out[block_rows, cols], product[:, cols])
-            if b < n_blocks - 1:
-                nc.sync.dma_start(out[block_rows, :], product[:])
+                end = start + piece
+                piece_offsets = offsets[:, start // ENTRIES_PER_OFFSET_COLUMN : end // ENTRIES_PER_OFFSET_COLUMN]
+                nc.scalar.activation(gate[:, start:end], tables[b][:].indirect(piece_offsets), TANH)
+                nc.vector.tensor_tensor(
+                    product[:, start:end],
+                    gate[:, start:end],
+                    stream[:, stream_start + start : stream_start + end],
+                    MULT,
+                )
+                if is_last:
+                    nc.sync.dma_start(out_rows[:, b * n + start : b * n + end], product[:, start:end])
+            if not is_last:
+                nc.sync.dma_start(out_rows[:, b * n : (b + 1) * n], product[:])

import concourse.mybir as mybir

P = 128
PIECE = 1024
LAST_PIECE = PIECE // 2
ENTRIES_PER_OFFSET_COLUMN = 16
BLOCKS_PER_PAIR = 2

TANH = mybir.ActivationFunctionType.Tanh
MULT = mybir.AluOpType.mult


def tile_lookup_gate_tanh_out_kernel(tc, tab, y, offs, out):
    nc = tc.nc
    rows, table_columns = tab.shape
    n = y.shape[1]
    n_blocks = rows // P
    n_pairs = n_blocks // BLOCKS_PER_PAIR
    f32 = mybir.dt.float32

    tab_rows = tab.rearrange("(p b) c -> p (b c)", b=n_blocks)
    y_rows = y.rearrange("(p b) c -> p (b c)", b=n_blocks)
    out_rows = out.rearrange("(p b) c -> p (b c)", b=n_blocks)

    with (
        tc.tile_pool(name="lists", bufs=1) as lists,
        tc.tile_pool(name="blocks", bufs=n_blocks) as blocks,
        tc.tile_pool(name="pairs", bufs=n_pairs) as pairs,
    ):
        offsets = lists.tile([P, n // ENTRIES_PER_OFFSET_COLUMN], mybir.dt.uint16, name="offsets")
        nc.sync.dma_start(offsets[:], offs)

        tables, streams = [], []
        for pair in range(n_pairs):
            for b in range(pair * BLOCKS_PER_PAIR, (pair + 1) * BLOCKS_PER_PAIR):
                table = blocks.tile([P, table_columns], f32, name="table")
                nc.sync.dma_start(table[:], tab_rows[:, b * table_columns : (b + 1) * table_columns])
                tables.append(table)
            stream = pairs.tile([P, BLOCKS_PER_PAIR * n], f32, name="stream")
            pair_columns = slice(pair * BLOCKS_PER_PAIR * n, (pair + 1) * BLOCKS_PER_PAIR * n)
            nc.sync.dma_start(stream[:], y_rows[:, pair_columns])
            streams.append(stream)

        for b in range(n_blocks):
            gate = blocks.tile([P, n], f32, name="gate")
            product = blocks.tile([P, n], f32, name="product")
            stream = streams[b // BLOCKS_PER_PAIR]
            stream_start = (b % BLOCKS_PER_PAIR) * n
            is_last = b == n_blocks - 1
            piece = LAST_PIECE if is_last else PIECE
            for start in range(0, n, piece):
                end = start + piece
                piece_offsets = offsets[:, start // ENTRIES_PER_OFFSET_COLUMN : end // ENTRIES_PER_OFFSET_COLUMN]
                nc.scalar.activation(gate[:, start:end], tables[b][:].indirect(piece_offsets), TANH)
                nc.vector.tensor_tensor(
                    product[:, start:end],
                    gate[:, start:end],
                    stream[:, stream_start + start : stream_start + end],
                    MULT,
                )
                if is_last:
                    nc.sync.dma_start(out_rows[:, b * n + start : b * n + end], product[:, start:end])
            if not is_last:
                nc.sync.dma_start(out_rows[:, b * n : (b + 1) * n], product[:])
